import numpy as np
import ml_dtypes


def mxq(x, axis, fmt="e4m3"):
    dtype, down = {"e4m3": (ml_dtypes.float8_e4m3fn, 7), "e5m2": (ml_dtypes.float8_e5m2, 14)}[fmt]
    v = np.moveaxis(np.asarray(x, np.float32).astype(ml_dtypes.bfloat16).astype(np.float64), axis, -1)
    blocks = v.reshape(v.shape[:-1] + (-1, 32))
    amax = np.abs(blocks).max(-1, keepdims=True)
    byte = np.maximum(np.where(amax > 0, np.frexp(amax)[1] - 1 + 127, 0) - down, 1)
    scale = np.exp2(byte - 127.0)
    codes = (blocks / scale).astype(np.float32).astype(dtype).astype(np.float64)
    return np.moveaxis((codes * scale).reshape(v.shape), -1, axis)


WIDE = False


def mx_kscale(k):
    if not WIDE:
        return np.ones(k)
    levels = np.array([10, -10, 5, -5, 0])
    if k % 512:
        return np.exp2(np.random.permutation(np.resize(levels, k // 32))).repeat(32)
    a = np.empty((k // 512, 16))
    for p in range(k // 512):
        a[p, :8] = np.random.permutation(np.resize(levels, 8))
        for g in range(8):
            far = levels[np.abs(levels - a[p, g]) >= 10]
            a[p, g + 8] = far[np.random.randint(len(far))]
    return np.exp2(a.ravel()).repeat(32)


def f64(x):
    return np.asarray(x).astype(np.float64)


def striped(idx):
    return np.tile(np.asarray(idx).reshape(-1, 16).T, (8, 1)).astype(np.uint16)


def unstriped(offs):
    return offs[:16].T.reshape(-1).astype(np.int64)


B, N, T, D, DV, NQ = 1, 1024, 2048, 512, 512, 256


def setup_inputs():
    n = np.random.standard_normal
    idx = np.random.permutation(T)[:B * N]
    u = mx_kscale(B * N)
    ut = np.ones(T)
    ut[idx] = u
    w = np.exp(n((B, N, NQ)))
    w = w / w.sum(1, keepdims=True)
    return {
        "wT": (w * u.reshape(B, N, 1)).astype(np.float32),
        "vT": (n((DV, T)) / ut).astype(np.float32),
        "offs": striped(idx),
    }


def reference(wT, vT, offs):
    idx = unstriped(offs)
    pick = lambda x: x[:, idx].reshape(x.shape[0], B, N).transpose(1, 0, 2)
    return mxq(f64(wT), 1, "e4m3").transpose(0, 2, 1) @ mxq(pick(f64(vT)).transpose(0, 2, 1), 1, "e4m3")

@@ -1,0 +1,176 @@
+from contextlib import ExitStack
+
+import concourse.mybir as mybir
+from concourse.masks import make_identity
+
+F32 = mybir.dt.float32
+BF16 = mybir.dt.bfloat16
+U32 = mybir.dt.uint32
+U16 = mybir.dt.uint16
+U8 = mybir.dt.uint8
+FP8X4 = mybir.dt.float8_e4m3fn_x4
+COPY = mybir.ActivationFunctionType.Copy
+
+P = 128
+T, E, NQ, SLOTS = 2048, 512, 256, 1024
+PASS = 512
+PASSES = SLOTS // PASS
+BLOCKS = E // P
+MT = NQ // P
+FLOPS = 2 * SLOTS * NQ * E
+HALF = T // 2
+
+CHUNKS = (2, 2, 2, 2)
+LOADS = (("b", 0), ("b", 1), ("b", 2), ("w", 0), ("b", 3), ("w", 1))
+
+
+def tile_attend_spmm_kernel(tc, wT, vT, offs, out):
+    nc = tc.nc
+    with ExitStack() as ctx:
+        keep = ctx.enter_context(tc.tile_pool(name="keep", bufs=1))
+        work = ctx.enter_context(tc.tile_pool(name="work", bufs=4))
+        turn = ctx.enter_context(tc.psum_pool(name="turn", bufs=4))
+        sums = ctx.enter_context(tc.psum_pool(name="sums", bufs=4))
+
+        offsets = keep.tile([P, SLOTS // 16], U16, name="offsets")
+        nc.sync.dma_start(offsets[:], offs)
+        w_raw = keep.tile([P, PASSES, 4, NQ], F32, name="w_raw")
+        w_hbm = wT.rearrange("b (g p j) q -> p (b g) j q", g=PASSES, j=4)
+        pools = [keep.tile([P, T], F32, name=f"pool{b}") for b in range(BLOCKS)]
+        for kind, i in LOADS:
+            if kind == "w":
+                nc.sync.dma_start(w_raw[:, i], w_hbm[:, i])
+            else:
+                n = CHUNKS[i]
+                for c in range(n):
+                    cols = slice(c * T // n, (c + 1) * T // n)
+                    nc.sync.dma_start(pools[i][:, cols], vT[i * P : (i + 1) * P, cols])
+
+        ident = keep.tile([P, P], F32, name="ident")
+        make_identity(nc, ident[:])
+        windows, turned, grouped, codes, scales, totals = {}, {}, {}, {}, {}, {}
+        picked = {}
+        staged = keep.tile([P, MT, E], F32, name="staged")
+        for b in range(BLOCKS):
+            turned[b] = turn.tile([P, PASSES, 2, P], F32, name="turned")
+            grouped[b] = keep.tile([P, PASSES * P * 4], BF16, align_bytes=64, name=f"grouped{b}")
+            codes[b] = keep.tile([P, PASSES * P], U32, align_bytes=64, name=f"codes{b}")
+            scales[b] = keep.tile([P, PASSES * P], U8, align_bytes=64, name=f"scales{b}")
+            totals[b] = sums.tile([P, MT, P], F32, name="total")
+            picked[b] = keep.tile([P, SLOTS], BF16, name=f"picked{b}")
+
+        w_grouped = keep.tile([P, PASSES, NQ, 4], BF16, align_bytes=64, name="w_grouped")
+        w_codes = keep.tile([P, PASSES, NQ], U32, align_bytes=64, name="w_codes")
+        w_scales = keep.tile([P, PASSES, NQ], U8, align_bytes=64, name="w_scales")
+
+        def lay_weights(g, engine="V"):
+            ins = w_raw[:, g].rearrange("p j q -> p q j")
+            if engine == "V":
+                nc.vector.tensor_copy(w_grouped[:, g], ins)
+            else:
+                nc.scalar.activation(w_grouped[:, g], ins, COPY)
+
+        def quantize_weights(g):
+            nc.vector.quantize_mx(
+                out=w_codes[:, g].bitcast(FP8X4),
+                scales=w_scales[:, g],
+                in_=w_grouped[:, g].rearrange("p q j -> p (q j)"),
+            )
+
+        def cast(b, c, engine="S"):
+            if b not in windows:
+                windows[b] = keep.tile([P, T], BF16, name=f"window{b}")
+            n = CHUNKS[b]
+            cols = slice(c * T // n, (c + 1) * T // n)
+            if engine == "V":
+                nc.vector.tensor_copy(windows[b][:, cols], pools[b][:, cols])
+            else:
+                nc.scalar.activation(windows[b][:, cols], pools[b][:, cols], COPY)
+
+        def gather(b, lo=0, hi=SLOTS, scalar=False):
+            place = picked[b][:].rearrange("p (u j h) -> p j u h", u=2, h=2)[:, lo // 4 : hi // 4]
+            listed = offsets[:, lo // 16 : hi // 16]
+            if scalar:
+                nc.scalar.activation(place, windows[b][:].indirect(listed), COPY)
+            else:
+                nc.vector.tensor_copy(place, pools[b][:].indirect(listed))
+
+        def turn_words(b, g):
+            words = picked[b][:].bitcast(F32)
+            for u in range(2):
+                i = u * PASSES + g
+                nc.tensor.transpose(turned[b][:, g, u, :], words[:, i * P : (i + 1) * P], ident[:])
+
+        def copy_out(engine, b, g0=0, g1=PASSES):
+            place = grouped[b][:].bitcast(F32).rearrange("p (g e u) -> p g e u", g=PASSES, u=2)
+            copy = nc.vector.tensor_copy if engine == "V" else nc.scalar.copy
+            copy(place[:, g0:g1], turned[b][:, g0:g1].rearrange("p g u e -> p g e u"))
+
+        def quantize(b, g0=0, g1=PASSES):
+            nc.vector.quantize_mx(
+                out=codes[b][:, g0 * P : g1 * P].bitcast(FP8X4),
+                scales=scales[b][:, g0 * P : g1 * P],
+                in_=grouped[b][:, g0 * 4 * P : g1 * 4 * P],
+            )
+
+        def multiply(b):
+            for m in range(MT):
+                q_cols = slice(m * P, (m + 1) * P)
+                for g in range(PASSES):
+                    e_cols = slice(g * P, (g + 1) * P)
+                    nc.tensor.matmul_mx(
+                        out=totals[b][:, m, :],
+                        lhsT=w_codes[:, g, q_cols].bitcast(FP8X4),
+                        lhsT_scale=w_scales[:, g, q_cols],
+                        rhs=codes[b][:, e_cols].bitcast(FP8X4),
+                        rhs_scale=scales[b][:, e_cols],
+                        start=(g == 0),
+                        stop=(g == PASSES - 1),
+                    )
+
+        def stage(engine, b):
+            copy = nc.vector.tensor_copy if engine == "V" else nc.scalar.copy
+            copy(staged[:, :, b * P : (b + 1) * P], totals[b][:])
+
+        out_hbm = out.rearrange("b (m q) e -> q (b m) e", m=MT)
+
+        def store(b0, b1):
+            nc.sync.dma_start(out_hbm[:, :, b0 * P : b1 * P], staged[:, :, b0 * P : b1 * P])
+
+        gather(0)
+        turn_words(0, 0)
+        turn_words(0, 1)
+        copy_out("S", 0)
+        gather(1)
+        turn_words(1, 0)
+        turn_words(1, 1)
+        quantize(0)
+        copy_out("S", 1)
+        gather(2)
+        turn_words(2, 0)
+        turn_words(2, 1)
+        lay_weights(0, "S")
+        quantize(1)
+        copy_out("S", 2)
+        quantize_weights(0)
+        gather(3, 0, 512)
+        turn_words(3, 0)
+        quantize(2)
+        gather(3, 512, 1024)
+        turn_words(3, 1)
+        lay_weights(1, "S")
+        copy_out("S", 3, 0, 1)
+        copy_out("S", 3, 1, 2)
+        quantize_weights(1)
+        multiply(0)
+        multiply(1)
+        quantize(3, 0, 1)
+        quantize(3, 1, 2)
+        multiply(2)
+        stage("S", 0)
+        stage("V", 1)
+        multiply(3)
+        stage("S", 2)
+        store(0, 3)
+        stage("V", 3)
+        store(3, 4)

@@ -28,67 +28,67 @@ def tile_attend_spmm_kernel(tc, wT, vT, offs, out):
     nc = tc.nc
     with ExitStack() as ctx:
         keep = ctx.enter_context(tc.tile_pool(name="keep", bufs=1))
-        work = ctx.enter_context(tc.tile_pool(name="work", bufs=4))
-        turn = ctx.enter_context(tc.psum_pool(name="turn", bufs=4))
-        sums = ctx.enter_context(tc.psum_pool(name="sums", bufs=4))
+        turn = ctx.enter_context(tc.psum_pool(name="turn", bufs=1))
+        sums = ctx.enter_context(tc.psum_pool(name="sums", bufs=1))
 
         offsets = keep.tile([P, SLOTS // 16], U16, name="offsets")
         nc.sync.dma_start(offsets[:], offs)
-        w_raw = keep.tile([P, PASSES, 4, NQ], F32, name="w_raw")
+        w_raw = [keep.tile([P, 4, NQ], F32, name=f"w_raw{g}") for g in range(PASSES)]
         w_hbm = wT.rearrange("b (g p j) q -> p (b g) j q", g=PASSES, j=4)
         pools = [keep.tile([P, T], F32, name=f"pool{b}") for b in range(BLOCKS)]
         for kind, i in LOADS:
             if kind == "w":
-                nc.sync.dma_start(w_raw[:, i], w_hbm[:, i])
+                nc.sync.dma_start(w_raw[i][:], w_hbm[:, i])
             else:
-                n = CHUNKS[i]
-                for c in range(n):
-                    cols = slice(c * T // n, (c + 1) * T // n)
-                    nc.sync.dma_start(pools[i][:, cols], vT[i * P : (i + 1) * P, cols])
+                nc.sync.dma_start(pools[i][:], vT[i * P : (i + 1) * P, :])
 
         ident = keep.tile([P, P], F32, name="ident")
         make_identity(nc, ident[:])
-        windows, turned, grouped, codes, scales, totals = {}, {}, {}, {}, {}, {}
-        picked = {}
-        staged = keep.tile([P, MT, E], F32, name="staged")
-        for b in range(BLOCKS):
-            turned[b] = turn.tile([P, PASSES, 2, P], F32, name="turned")
-            grouped[b] = keep.tile([P, PASSES * P * 4], BF16, align_bytes=64, name=f"grouped{b}")
-            codes[b] = keep.tile([P, PASSES * P], U32, align_bytes=64, name=f"codes{b}")
-            scales[b] = keep.tile([P, PASSES * P], U8, align_bytes=64, name=f"scales{b}")
-            totals[b] = sums.tile([P, MT, P], F32, name="total")
+        windows = {}
+        picked, turned = {}, {}
+        for b in range(3):
             picked[b] = keep.tile([P, SLOTS], BF16, name=f"picked{b}")
+        for g in range(PASSES):
+            picked[3, g] = keep.tile([P, PASS], BF16, name=f"picked3{g}")
+        banks = [turn.tile([P, 512], F32, name=f"bank{i}") for i in range(4)]
+        totals = {(m, h): sums.tile([P, E // 2], F32, name=f"total{m}{h}") for m in range(MT) for h in range(2)}
+        grouped = keep.tile([P, PASSES, E, 4], BF16, align_bytes=64, name="grouped")
+        codes = [keep.tile([P, E], U32, align_bytes=64, name=f"codes{g}") for g in range(PASSES)]
+        scales = [keep.tile([P, E], U8, align_bytes=64, name=f"scales{g}") for g in range(PASSES)]
+        staged = {(m, h): keep.tile([P, E // 2], F32, name=f"staged{m}{h}") for m in range(MT) for h in range(2)}
+        w_grouped = [keep.tile([P, NQ, 4], BF16, align_bytes=64, name=f"w_grouped{g}") for g in range(PASSES)]
+        w_codes = [keep.tile([P, NQ], U32, align_bytes=64, name=f"w_codes{g}") for g in range(PASSES)]
+        w_scales = [keep.tile([P, NQ], U8, align_bytes=64, name=f"w_scales{g}") for g in range(PASSES)]
 
-        w_grouped = keep.tile([P, PASSES, NQ, 4], BF16, align_bytes=64, name="w_grouped")
-        w_codes = keep.tile([P, PASSES, NQ], U32, align_bytes=64, name="w_codes")
-        w_scales = keep.tile([P, PASSES, NQ], U8, align_bytes=64, name="w_scales")
-
-        def lay_weights(g, engine="V"):
-            ins = w_raw[:, g].rearrange("p j q -> p q j")
+        def copy(engine, to, source):
             if engine == "V":
-                nc.vector.tensor_copy(w_grouped[:, g], ins)
+                nc.vector.tensor_copy(to, source)
+            elif engine == "G":
+                nc.gpsimd.tensor_scalar(to, source, 1.0, 0.0, mybir.AluOpType.mult, mybir.AluOpType.add)
             else:
-                nc.scalar.activation(w_grouped[:, g], ins, COPY)
+                nc.scalar.activation(to, source, COPY)
+
+        def lay_weights(g, m, engine):
+            q = slice(0, NQ) if m == 2 else slice(m * P, (m + 1) * P)
+            copy(engine, w_grouped[g][:, q], w_raw[g][:, :, q].rearrange("p j q -> p q j"))
 
         def quantize_weights(g):
             nc.vector.quantize_mx(
-                out=w_codes[:, g].bitcast(FP8X4),
-                scales=w_scales[:, g],
-                in_=w_grouped[:, g].rearrange("p q j -> p (q j)"),
+                out=w_codes[g][:].bitcast(FP8X4),
+                scales=w_scales[g][:],
+                in_=w_grouped[g][:].rearrange("p q j -> p (q j)"),
             )
 
-        def cast(b, c, engine="S"):
+        def cast(b, c, engine):
             if b not in windows:
                 windows[b] = keep.tile([P, T], BF16, name=f"window{b}")
             n = CHUNKS[b]
             cols = slice(c * T // n, (c + 1) * T // n)
-            if engine == "V":
-                nc.vector.tensor_copy(windows[b][:, cols], pools[b][:, cols])
-            else:
-                nc.scalar.activation(windows[b][:, cols], pools[b][:, cols], COPY)
+            copy(engine, windows[b][:, cols], pools[b][:, cols])
 
         def gather(b, lo=0, hi=SLOTS, scalar=False):
-            place = picked[b][:].rearrange("p (u j h) -> p j u h", u=2, h=2)[:, lo // 4 : hi // 4]
+            tile = picked[b] if b < 3 else picked[b, lo // PASS]
+            place = tile[:].rearrange("p (u j h) -> p j u h", u=2, h=2)
             listed = offsets[:, lo // 16 : hi // 16]
             if scalar:
                 nc.scalar.activation(place, windows[b][:].indirect(listed), COPY)
@@ -96,81 +96,93 @@ def tile_attend_spmm_kernel(tc, wT, vT, offs, out):
                 nc.vector.tensor_copy(place, pools[b][:].indirect(listed))
 
         def turn_words(b, g):
-            words = picked[b][:].bitcast(F32)
+            words = (picked[b] if b < 3 else picked[b, g])[:].bitcast(F32)
+            bank = banks[b] if b < 3 else banks[3 if g == 0 else 0]
             for u in range(2):
-                i = u * PASSES + g
-                nc.tensor.transpose(turned[b][:, g, u, :], words[:, i * P : (i + 1) * P], ident[:])
+                i = u * PASSES + g if b < 3 else u
+                k = 2 * g + u if b < 3 else u
+                nc.tensor.transpose(bank[:, k * P : (k + 1) * P], words[:, i * P : (i + 1) * P], ident[:])
 
         def copy_out(engine, b, g0=0, g1=PASSES):
-            place = grouped[b][:].bitcast(F32).rearrange("p (g e u) -> p g e u", g=PASSES, u=2)
-            copy = nc.vector.tensor_copy if engine == "V" else nc.scalar.copy
-            copy(place[:, g0:g1], turned[b][:, g0:g1].rearrange("p g u e -> p g e u"))
+            place = grouped[:, g0:g1, b * P : (b + 1) * P].bitcast(F32)
+            bank = banks[b] if b < 3 else banks[3 if g0 == 0 else 0]
+            source = bank[:, 0 : 2 * (g1 - g0) * P].rearrange("p (g u e) -> p g e u", u=2, e=P)
+            if engine == "V":
+                nc.vector.tensor_copy(place, source)
+            else:
+                nc.scalar.copy(place, source)
 
-        def quantize(b, g0=0, g1=PASSES):
+        def quantize(b0, b1, g):
+            cols = slice(b0 * P, b1 * P)
             nc.vector.quantize_mx(
-                out=codes[b][:, g0 * P : g1 * P].bitcast(FP8X4),
-                scales=scales[b][:, g0 * P : g1 * P],
-                in_=grouped[b][:, g0 * 4 * P : g1 * 4 * P],
+                out=codes[g][:, cols].bitcast(FP8X4),
+                scales=scales[g][:, cols],
+                in_=grouped[:, g, cols].rearrange("p e t -> p (e t)"),
             )
 
-        def multiply(b):
-            for m in range(MT):
-                q_cols = slice(m * P, (m + 1) * P)
-                for g in range(PASSES):
-                    e_cols = slice(g * P, (g + 1) * P)
-                    nc.tensor.matmul_mx(
-                        out=totals[b][:, m, :],
-                        lhsT=w_codes[:, g, q_cols].bitcast(FP8X4),
-                        lhsT_scale=w_scales[:, g, q_cols],
-                        rhs=codes[b][:, e_cols].bitcast(FP8X4),
-                        rhs_scale=scales[b][:, e_cols],
-                        start=(g == 0),
-                        stop=(g == PASSES - 1),
-                    )
-
-        def stage(engine, b):
-            copy = nc.vector.tensor_copy if engine == "V" else nc.scalar.copy
-            copy(staged[:, :, b * P : (b + 1) * P], totals[b][:])
+        def multiply(g, m, h):
+            q_cols = slice(m * P, (m + 1) * P)
+            e_cols = slice(h * E // 2, (h + 1) * E // 2)
+            nc.tensor.matmul_mx(
+                out=totals[m, h][:],
+                lhsT=w_codes[g][:, q_cols].bitcast(FP8X4),
+                lhsT_scale=w_scales[g][:, q_cols],
+                rhs=codes[g][:, e_cols].bitcast(FP8X4),
+                rhs_scale=scales[g][:, e_cols],
+                start=(g == 0),
+                stop=(g == PASSES - 1),
+            )
 
         out_hbm = out.rearrange("b (m q) e -> q (b m) e", m=MT)
 
-        def store(b0, b1):
-            nc.sync.dma_start(out_hbm[:, :, b0 * P : b1 * P], staged[:, :, b0 * P : b1 * P])
+        def stage(engine, m, h):
+            to = staged[m, h][:]
+            if engine == "V":
+                nc.vector.tensor_copy(to, totals[m, h][:])
+            else:
+                nc.scalar.copy(to, totals[m, h][:])
 
-        gather(0)
+        def store(m, h):
+            e_cols = slice(h * E // 2, (h + 1) * E // 2)
+            nc.sync.dma_start(out_hbm[:, m, e_cols], staged[m, h][:])
+
+        gather(0, 0, 1024)
         turn_words(0, 0)
         turn_words(0, 1)
-        copy_out("S", 0)
-        gather(1)
+        copy_out("S", 0, 0, 2)
+        gather(1, 0, 1024)
         turn_words(1, 0)
         turn_words(1, 1)
-        quantize(0)
-        copy_out("S", 1)
-        gather(2)
+        copy_out("S", 1, 0, 2)
+        lay_weights(0, 2, "G")
+        gather(2, 0, 1024)
         turn_words(2, 0)
         turn_words(2, 1)
-        lay_weights(0, "S")
-        quantize(1)
-        copy_out("S", 2)
-        quantize_weights(0)
+        copy_out("S", 2, 0, 2)
         gather(3, 0, 512)
         turn_words(3, 0)
-        quantize(2)
         gather(3, 512, 1024)
         turn_words(3, 1)
-        lay_weights(1, "S")
         copy_out("S", 3, 0, 1)
-        copy_out("S", 3, 1, 2)
+        lay_weights(1, 2, "G")
+        quantize_weights(0)
+        quantize(0, 4, 0)
         quantize_weights(1)
-        multiply(0)
-        multiply(1)
-        quantize(3, 0, 1)
-        quantize(3, 1, 2)
-        multiply(2)
-        stage("S", 0)
-        stage("V", 1)
-        multiply(3)
-        stage("S", 2)
-        store(0, 3)
-        stage("V", 3)
-        store(3, 4)
+        copy_out("S", 3, 1, 2)
+        quantize(0, 4, 1)
+        multiply(0, 0, 0)
+        multiply(0, 0, 1)
+        multiply(0, 1, 0)
+        multiply(0, 1, 1)
+        multiply(1, 0, 0)
+        multiply(1, 0, 1)
+        multiply(1, 1, 0)
+        multiply(1, 1, 1)
+        stage("V", 0, 0)
+        store(0, 0)
+        stage("S", 0, 1)
+        store(0, 1)
+        stage("V", 1, 0)
+        store(1, 0)
+        stage("S", 1, 1)
+        store(1, 1)

from contextlib import ExitStack

import concourse.mybir as mybir
from concourse.masks import make_identity

F32 = mybir.dt.float32
BF16 = mybir.dt.bfloat16
U32 = mybir.dt.uint32
U16 = mybir.dt.uint16
U8 = mybir.dt.uint8
FP8X4 = mybir.dt.float8_e4m3fn_x4
COPY = mybir.ActivationFunctionType.Copy

P = 128
T, E, NQ, SLOTS = 2048, 512, 256, 1024
PASS = 512
PASSES = SLOTS // PASS
BLOCKS = E // P
MT = NQ // P
FLOPS = 2 * SLOTS * NQ * E
HALF = T // 2

CHUNKS = (2, 2, 2, 2)
LOADS = (("b", 0), ("b", 1), ("b", 2), ("w", 0), ("b", 3), ("w", 1))


def tile_attend_spmm_kernel(tc, wT, vT, offs, out):
    nc = tc.nc
    with ExitStack() as ctx:
        keep = ctx.enter_context(tc.tile_pool(name="keep", bufs=1))
        turn = ctx.enter_context(tc.psum_pool(name="turn", bufs=1))
        sums = ctx.enter_context(tc.psum_pool(name="sums", bufs=1))

        offsets = keep.tile([P, SLOTS // 16], U16, name="offsets")
        nc.sync.dma_start(offsets[:], offs)
        w_raw = [keep.tile([P, 4, NQ], F32, name=f"w_raw{g}") for g in range(PASSES)]
        w_hbm = wT.rearrange("b (g p j) q -> p (b g) j q", g=PASSES, j=4)
        pools = [keep.tile([P, T], F32, name=f"pool{b}") for b in range(BLOCKS)]
        for kind, i in LOADS:
            if kind == "w":
                nc.sync.dma_start(w_raw[i][:], w_hbm[:, i])
            else:
                nc.sync.dma_start(pools[i][:], vT[i * P : (i + 1) * P, :])

        ident = keep.tile([P, P], F32, name="ident")
        make_identity(nc, ident[:])
        windows = {}
        picked, turned = {}, {}
        for b in range(3):
            picked[b] = keep.tile([P, SLOTS], BF16, name=f"picked{b}")
        for g in range(PASSES):
            picked[3, g] = keep.tile([P, PASS], BF16, name=f"picked3{g}")
        banks = [turn.tile([P, 512], F32, name=f"bank{i}") for i in range(4)]
        totals = {(m, h): sums.tile([P, E // 2], F32, name=f"total{m}{h}") for m in range(MT) for h in range(2)}
        grouped = keep.tile([P, PASSES, E, 4], BF16, align_bytes=64, name="grouped")
        codes = [keep.tile([P, E], U32, align_bytes=64, name=f"codes{g}") for g in range(PASSES)]
        scales = [keep.tile([P, E], U8, align_bytes=64, name=f"scales{g}") for g in range(PASSES)]
        staged = {(m, h): keep.tile([P, E // 2], F32, name=f"staged{m}{h}") for m in range(MT) for h in range(2)}
        w_grouped = [keep.tile([P, NQ, 4], BF16, align_bytes=64, name=f"w_grouped{g}") for g in range(PASSES)]
        w_codes = [keep.tile([P, NQ], U32, align_bytes=64, name=f"w_codes{g}") for g in range(PASSES)]
        w_scales = [keep.tile([P, NQ], U8, align_bytes=64, name=f"w_scales{g}") for g in range(PASSES)]

        def copy(engine, to, source):
            if engine == "V":
                nc.vector.tensor_copy(to, source)
            elif engine == "G":
                nc.gpsimd.tensor_scalar(to, source, 1.0, 0.0, mybir.AluOpType.mult, mybir.AluOpType.add)
            else:
                nc.scalar.activation(to, source, COPY)

        def lay_weights(g, m, engine):
            q = slice(0, NQ) if m == 2 else slice(m * P, (m + 1) * P)
            copy(engine, w_grouped[g][:, q], w_raw[g][:, :, q].rearrange("p j q -> p q j"))

        def quantize_weights(g):
            nc.vector.quantize_mx(
                out=w_codes[g][:].bitcast(FP8X4),
                scales=w_scales[g][:],
                in_=w_grouped[g][:].rearrange("p q j -> p (q j)"),
            )

        def cast(b, c, engine):
            if b not in windows:
                windows[b] = keep.tile([P, T], BF16, name=f"window{b}")
            n = CHUNKS[b]
            cols = slice(c * T // n, (c + 1) * T // n)
            copy(engine, windows[b][:, cols], pools[b][:, cols])

        def gather(b, lo=0, hi=SLOTS, scalar=False):
            tile = picked[b] if b < 3 else picked[b, lo // PASS]
            place = tile[:].rearrange("p (u j h) -> p j u h", u=2, h=2)
            listed = offsets[:, lo // 16 : hi // 16]
            if scalar:
                nc.scalar.activation(place, windows[b][:].indirect(listed), COPY)
            else:
                nc.vector.tensor_copy(place, pools[b][:].indirect(listed))

        def turn_words(b, g):
            words = (picked[b] if b < 3 else picked[b, g])[:].bitcast(F32)
            bank = banks[b] if b < 3 else banks[3 if g == 0 else 0]
            for u in range(2):
                i = u * PASSES + g if b < 3 else u
                k = 2 * g + u if b < 3 else u
                nc.tensor.transpose(bank[:, k * P : (k + 1) * P], words[:, i * P : (i + 1) * P], ident[:])

        def copy_out(engine, b, g0=0, g1=PASSES):
            place = grouped[:, g0:g1, b * P : (b + 1) * P].bitcast(F32)
            bank = banks[b] if b < 3 else banks[3 if g0 == 0 else 0]
            source = bank[:, 0 : 2 * (g1 - g0) * P].rearrange("p (g u e) -> p g e u", u=2, e=P)
            if engine == "V":
                nc.vector.tensor_copy(place, source)
            else:
                nc.scalar.copy(place, source)

        def quantize(b0, b1, g):
            cols = slice(b0 * P, b1 * P)
            nc.vector.quantize_mx(
                out=codes[g][:, cols].bitcast(FP8X4),
                scales=scales[g][:, cols],
                in_=grouped[:, g, cols].rearrange("p e t -> p (e t)"),
            )

        def multiply(g, m, h):
            q_cols = slice(m * P, (m + 1) * P)
            e_cols = slice(h * E // 2, (h + 1) * E // 2)
            nc.tensor.matmul_mx(
                out=totals[m, h][:],
                lhsT=w_codes[g][:, q_cols].bitcast(FP8X4),
                lhsT_scale=w_scales[g][:, q_cols],
                rhs=codes[g][:, e_cols].bitcast(FP8X4),
                rhs_scale=scales[g][:, e_cols],
                start=(g == 0),
                stop=(g == PASSES - 1),
            )

        out_hbm = out.rearrange("b (m q) e -> q (b m) e", m=MT)

        def stage(engine, m, h):
            to = staged[m, h][:]
            if engine == "V":
                nc.vector.tensor_copy(to, totals[m, h][:])
            else:
                nc.scalar.copy(to, totals[m, h][:])

        def store(m, h):
            e_cols = slice(h * E // 2, (h + 1) * E // 2)
            nc.sync.dma_start(out_hbm[:, m, e_cols], staged[m, h][:])

        gather(0, 0, 1024)
        turn_words(0, 0)
        turn_words(0, 1)
        copy_out("S", 0, 0, 2)
        gather(1, 0, 1024)
        turn_words(1, 0)
        turn_words(1, 1)
        copy_out("S", 1, 0, 2)
        lay_weights(0, 2, "G")
        gather(2, 0, 1024)
        turn_words(2, 0)
        turn_words(2, 1)
        copy_out("S", 2, 0, 2)
        gather(3, 0, 512)
        turn_words(3, 0)
        gather(3, 512, 1024)
        turn_words(3, 1)
        copy_out("S", 3, 0, 1)
        lay_weights(1, 2, "G")
        quantize_weights(0)
        quantize(0, 4, 0)
        quantize_weights(1)
        copy_out("S", 3, 1, 2)
        quantize(0, 4, 1)
        multiply(0, 0, 0)
        multiply(0, 0, 1)
        multiply(0, 1, 0)
        multiply(0, 1, 1)
        multiply(1, 0, 0)
        multiply(1, 0, 1)
        multiply(1, 1, 0)
        multiply(1, 1, 1)
        stage("V", 0, 0)
        store(0, 0)
        stage("S", 0, 1)
        store(0, 1)
        stage("V", 1, 0)
        store(1, 0)
        stage("S", 1, 1)
        store(1, 1)
